import numpy as np
import ml_dtypes


def mxq(x, axis, fmt="e4m3"):
    dtype, down = {"e4m3": (ml_dtypes.float8_e4m3fn, 7), "e5m2": (ml_dtypes.float8_e5m2, 14)}[fmt]
    v = np.moveaxis(np.asarray(x, np.float32).astype(ml_dtypes.bfloat16).astype(np.float64), axis, -1)
    blocks = v.reshape(v.shape[:-1] + (-1, 32))
    amax = np.abs(blocks).max(-1, keepdims=True)
    byte = np.maximum(np.where(amax > 0, np.frexp(amax)[1] - 1 + 127, 0) - down, 1)
    scale = np.exp2(byte - 127.0)
    codes = (blocks / scale).astype(np.float32).astype(dtype).astype(np.float64)
    return np.moveaxis((codes * scale).reshape(v.shape), -1, axis)


WIDE = False


def mx_kscale(k):
    if not WIDE:
        return np.ones(k)
    levels = np.array([10, -10, 5, -5, 0])
    if k % 512:
        return np.exp2(np.random.permutation(np.resize(levels, k // 32))).repeat(32)
    a = np.empty((k // 512, 16))
    for p in range(k // 512):
        a[p, :8] = np.random.permutation(np.resize(levels, 8))
        for g in range(8):
            far = levels[np.abs(levels - a[p, g]) >= 10]
            a[p, g + 8] = far[np.random.randint(len(far))]
    return np.exp2(a.ravel()).repeat(32)


BF16 = ml_dtypes.bfloat16


def bf(x):
    return np.asarray(x, np.float32).astype(BF16)


def f64(x):
    return np.asarray(x).astype(np.float64)


E2M1 = np.array([0.0, 0.5, 1.0, 1.5, 2.0, 3.0, 4.0, 6.0, -0.0, -0.5, -1.0, -1.5, -2.0, -3.0, -4.0, -6.0])


def pack_weight(w, fmt):
    k, n = w.shape
    w = f64(bf(w)).reshape(k // 32, 32, n)
    amax = np.abs(w).max(1)
    if fmt == "e4m3":
        byte = np.frexp(amax)[1] - 1 + 127 - 7
    else:
        mant, ex = np.frexp(amax / 6.0)
        byte = np.where(mant > 0.5, ex, ex - 1) + 127
    byte = np.clip(np.where(amax > 0, byte, 1), 1, 254)
    scaled = (w * np.exp2(127.0 - byte)[:, None, :]).reshape(k, n).astype(np.float32)
    by_word = np.ascontiguousarray(scaled.reshape(k // 512, 128, 4, n).transpose(0, 1, 3, 2))
    if fmt == "e4m3":
        words = by_word.astype(ml_dtypes.float8_e4m3fn).view(np.uint8)
    else:
        c = by_word.astype(ml_dtypes.float4_e2m1fn).view(np.uint8) & 0xF
        words = c[..., 0::2] | (c[..., 1::2] << 4)
    return np.ascontiguousarray(words), np.ascontiguousarray(byte.astype(np.uint8).reshape(k // 512, 16, n))


def unpack_weight(words, scales, fmt):
    g, p, n, _ = words.shape
    if fmt == "e4m3":
        vals = np.ascontiguousarray(words).view(ml_dtypes.float8_e4m3fn).astype(np.float64)
    else:
        nib = np.empty((g, p, n, 4), np.uint8)
        nib[..., 0::2] = words & 0xF
        nib[..., 1::2] = words >> 4
        vals = E2M1[nib]
    vals = vals * np.repeat(np.exp2(scales.astype(np.float64) - 127.0), 8, axis=1)[..., None]
    return vals.transpose(0, 1, 3, 2).reshape(g * 512, n)
def pack4(w):
    words, scales = pack_weight(w, "e2m1")
    return words.reshape(words.shape[0], 128, -1), scales


def unpack4(words, scales):
    return unpack_weight(words.reshape(words.shape[0], 128, -1, 2), scales, "e2m1")


D, R, C, J = 512, 8, 512, 512


def setup_inputs():
    s = mx_kscale(C)
    u = mx_kscale(D)
    t = mx_kscale(R * C)
    x = np.random.standard_normal((D, R * C)) * np.tile(s, R) * u[:, None]
    a = 0.35 * np.random.standard_normal((C, C)) / np.sqrt(C) / s[:, None] * s
    l = 0.35 * np.random.standard_normal((D, D)) / np.sqrt(D) / u[:, None] * u
    w = np.random.standard_normal((R * C, J)) / np.sqrt(R * C) / t[:, None]
    a_words, a_scales = pack4(a)
    l_words, l_scales = pack4(l)
    w_words, w_scales = pack4(w)
    return {"x": bf(x),
            "a_words": a_words, "a_scales": a_scales,
            "l_words": l_words, "l_scales": l_scales,
            "turnout": bf((0.4 + 0.5 * np.random.random(R * C)) * t / np.tile(s, R)),
            "w_words": w_words, "w_scales": w_scales,
            "electorate": bf((0.6 + 0.8 * np.random.random(D)) / u),
            "base": bf(0.3 * np.random.standard_normal(J))}


def reference(x, a_words, a_scales, l_words, l_scales, turnout, w_words, w_scales, electorate, base):
    x = f64(x)
    adj = mxq(x.reshape(D * R, C), 1, "e4m3") @ unpack4(a_words, a_scales)
    h = x + adj.reshape(D, R * C)
    v = h + (unpack4(l_words, l_scales).T @ mxq(h, 0, "e4m3"))
    z = v * f64(turnout)
    y = mxq(z, 1, "e4m3") @ unpack4(w_words, w_scales)
    return y * f64(electorate)[:, None] + f64(base)

@@ -1,0 +1,317 @@
+from contextlib import ExitStack
+
+import concourse.mybir as mybir
+from concourse.masks import make_identity
+
+D, R, C, J = 512, 8, 512, 512
+FLOPS = 3 * 2 * 512 * 512 * 4096
+
+F32 = mybir.dt.float32
+BF16 = mybir.dt.bfloat16
+I32 = mybir.dt.int32
+U32 = mybir.dt.uint32
+U8 = mybir.dt.uint8
+FP8X4 = mybir.dt.float8_e4m3fn_x4
+FP4X4 = mybir.dt.float4_e2m1fn_x4
+ADD = mybir.AluOpType.add
+MULT = mybir.AluOpType.mult
+COPY = mybir.ActivationFunctionType.Copy
+
+P = 128
+X_CHUNKS = ((0,), (1,), (2, 3), (4, 5), (6, 7))
+XT_ON_POOL = ()
+V_COLS = 512
+V_T = 2
+ORDER = "h0 H2 Z0 O0 P0 P1 P2 P3 A0 T0 h1 H3 Z1 O1 A1 h2 Z2 O2 N0 A2 T1 h3 Z3 O3 N1 A3 e Q G K X X X X"
+ORDER0 = "H0 H1 h0 u t H2 h1 q H3 T0 h2 N0 h3 N1 T1 X X X X G l Q"
+ORDER1 = "h0 H2 Z0 X T0 h1 H3 Z1 X h2 N0 Z2 X T1 h3 N1 Z3 X Q G"
+ORDER_R = "P0 P1 P2 P3 A0 A1 A2 A3 Z0 Z1 Z2 Z3 O0 O1 O2 O3 K X X X X"
+ORDER_T = "P0 P1 P2 P3 A0 A1 A2 A3 O0 O1 O2 O3 K"
+
+
+def tile_voting_intention_transfer_t2_kernel(
+    tc, x, a_words, a_scales, l_words, l_scales, turnout, w_words, w_scales, electorate, base, out
+):
+    nc = tc.nc
+    with ExitStack() as ctx:
+        keep = ctx.enter_context(tc.tile_pool(name="keep", bufs=1))
+        work = ctx.enter_context(tc.tile_pool(name="work", bufs=2))
+        psum = ctx.enter_context(tc.psum_pool(name="psum", bufs=1))
+
+        a_rsc = keep.tile([P, 512], U8, align_bytes=64)
+        l_rsc = keep.tile([P, 512], U8, align_bytes=64)
+        a_sc = keep.tile([P, 512], U8, align_bytes=64)
+        l_sc = keep.tile([P, 512], U8, align_bytes=64)
+        a_raw = keep.tile([P, 1024], U8, align_bytes=64)
+        l_raw = keep.tile([P, 1024], U8, align_bytes=64)
+        a_perm = keep.tile([P, 1024], U8, align_bytes=64)
+        l_perm = keep.tile([P, 1024], U8, align_bytes=64)
+        w_sb = keep.tile([P, R, 1024], U8, align_bytes=64)
+        w_sc = keep.tile([P, R, 512], U8, align_bytes=64)
+        tau_raw = keep.tile([P, R, 4], BF16)
+        tau = keep.tile([P, R * 4], F32)
+        elec_raw = keep.tile([P, 4], BF16)
+        elec = keep.tile([P, 4], F32)
+        base_sb = keep.tile([P, J], BF16)
+        ident = keep.tile([P, P], F32)
+        warm = keep.tile([P, 1], F32)
+
+        nc.vector.memset(a_rsc[:].bitcast(I32), 0)
+        nc.vector.memset(l_rsc[:].bitcast(I32), 0)
+        nc.vector.memset(warm[:], 0.0)
+        make_identity(nc, ident[:])
+        nc.gpsimd.memset(w_sc[:].rearrange("p g n -> p (g n)").bitcast(I32), 0)
+
+        x_view = {}
+
+        def load_x(chunk):
+            width = 512 * len(chunk)
+            xn = keep.tile([P, 4, width], BF16, name="x_rows%d" % chunk[0], align_bytes=64)
+            rows = x[:, 512 * chunk[0] : 512 * chunk[0] + width].rearrange("(p t) c -> p t c", t=4)
+            if chunk[0] == 0:
+                for h in range(2):
+                    nc.sync.dma_start(out=xn[:, 2 * h : 2 * h + 2, :], in_=rows[:, 2 * h : 2 * h + 2, :])
+            else:
+                nc.sync.dma_start(out=xn[:], in_=rows)
+            for n, r in enumerate(chunk):
+                x_view[r] = (xn, 512 * n)
+
+        def load_scales(dst, s):
+            for qd in range(4):
+                nc.sync.dma_start(
+                    out=dst[32 * qd : 32 * qd + 4, :].bitcast(I32), in_=s[0, 4 * qd : 4 * qd + 4, :].bitcast(I32)
+                )
+
+        nc.scalar.activation(out=warm[:], in_=warm[:], func=COPY, scale=1.0)
+        load_x(X_CHUNKS[0])
+        nc.sync.dma_start(out=a_raw[:], in_=a_words.rearrange("g p n -> p (g n)"))
+        load_scales(a_rsc, a_scales)
+        load_x(X_CHUNKS[1])
+        nc.sync.dma_start(out=tau_raw[:], in_=turnout.rearrange("(r p q) -> p r q", p=P, q=4))
+        load_x(X_CHUNKS[2])
+        nc.sync.dma_start(out=l_raw[:], in_=l_words.rearrange("g p n -> p (g n)"))
+        load_scales(l_rsc, l_scales)
+        for chunk in X_CHUNKS[3:]:
+            load_x(chunk)
+        nc.sync.dma_start(out=w_sb[:], in_=w_words.rearrange("g p n -> p g n"))
+        for qd in range(4):
+            nc.sync.dma_start(
+                out=w_sc[32 * qd : 32 * qd + 4, :, :].bitcast(I32),
+                in_=w_scales[:, 4 * qd : 4 * qd + 4, :].bitcast(I32).rearrange("g q n -> q g n"),
+            )
+        nc.sync.dma_start(out=elec_raw[:], in_=electorate.rearrange("(m t) -> m t", t=4))
+        nc.sync.dma_start(out=base_sb[:], in_=base.partition_broadcast(P))
+
+        xt, xq, xs, xtau, hg, hq, hs, zs, zg, zq, zsc, acc = {}, {}, {}, {}, {}, {}, {}, {}, {}, {}, {}, {}
+
+        def transpose(r):
+            xn, off = x_view[r]
+            xt[r] = keep.tile([P, 512, 4], BF16, name="xt%d" % r, align_bytes=64)
+            words = xn[:].bitcast(F32)
+            for b in range(2):
+                bank = psum.tile([P, 2, 2, P], F32, name="tp", tag="acc%d" % (2 * (r % 2) + b))
+                for t in range(2):
+                    for u in range(2):
+                        lo = off // 2
+                        nc.tensor.transpose(bank[:, t, u, :], words[:, 2 * b + t, lo + u : lo + 256 : 2], ident[:])
+                (nc.vector.tensor_copy if (r < V_T and b == 1) else nc.scalar.copy)(
+                    out=xt[r][:].bitcast(F32)[:, 256 * b : 256 * b + 256, :].rearrange("p (t m) u -> p t m u", t=2),
+                    in_=bank[:].rearrange("p t u m -> p t m u"),
+                )
+
+        def quantize(codes, scales, grouped, lo=0, hi=512):
+            nc.vector.quantize_mx(
+                out=codes[:, lo:hi].bitcast(FP8X4),
+                scales=scales[:, lo:hi],
+                in_=grouped[:, lo:hi, :].rearrange("p e t -> p (e t)"),
+            )
+
+        def quantize_x(r, parts=1):
+            xq[r] = keep.tile([P, 512], U32, name="xq%d" % r, align_bytes=64)
+            xs[r] = keep.tile([P, 512], U8, name="xs%d" % r, align_bytes=64)
+            for n in range(parts):
+                w = 512 // parts
+                quantize(xq[r], xs[r], xt[r], n * w, n * w + w)
+
+        def x_tau(r, q):
+            if q == 0:
+                xtau[r] = work.tile([P, 4, 512], F32, name="xtau", bufs=3, align_bytes=64)
+            k = 4 * r + q
+            if r in XT_ON_POOL:
+                nc.gpsimd.tensor_scalar(
+                    out=xtau[r][:, q, :], in0=xt[r][:, :, q], scalar1=tau[:, k : k + 1], scalar2=0.0, op0=MULT, op1=ADD
+                )
+            else:
+                nc.scalar.activation(out=xtau[r][:, q, :], in_=xt[r][:, :, q], func=COPY, scale=tau[:, k : k + 1])
+
+        banks = {}
+
+        def h_mm(r, q):
+            bank = psum.tile([P, 4, P], F32, name="hbank", tag="h", bufs=2)
+            banks[r, q] = bank
+            for t in range(4):
+                nc.tensor.matmul_mx(
+                    out=bank[:, t, :],
+                    lhsT=xq[r][:, P * t : P * t + P].bitcast(FP8X4),
+                    lhsT_scale=xs[r][:, P * t : P * t + P],
+                    rhs=a_perm[:, 256 * q : 256 * q + 256].bitcast(FP4X4),
+                    rhs_scale=a_sc[:, P * q : P * q + P],
+                    start=True,
+                    stop=True,
+                )
+
+        def h_add(r, q):
+            if q == 0:
+                hg[r] = work.tile([P, 512, 4], BF16, name="hg", align_bytes=64)
+            xn, off = x_view[r]
+            nc.vector.tensor_tensor(
+                out=hg[r][:, P * q : P * q + P, :].rearrange("p (c i) t -> p c t i", i=4),
+                in0=banks[r, q][:].rearrange("p t (c i) -> p c t i", i=4),
+                in1=xn[:, :, off : off + 512].rearrange("p t (c i q) -> p q c t i", q=4, i=4)[:, q],
+                op=ADD,
+            )
+
+        def quantize_h(r):
+            hq[r] = work.tile([P, 512], U32, name="hq", align_bytes=64)
+            hs[r] = work.tile([P, 512], U8, name="hs", align_bytes=64)
+            quantize(hq[r], hs[r], hg[r])
+
+        def z_mm(r, q):
+            bank = psum.tile([P, 512], F32, name="zbank", tag="z", bufs=2)
+            banks[r, q] = bank
+            nc.tensor.matmul_mx(
+                out=bank[:],
+                lhsT=a_perm[:, 256 * q : 256 * q + 256].bitcast(FP4X4),
+                lhsT_scale=a_sc[:, P * q : P * q + P],
+                rhs=xq[r][:].bitcast(FP8X4),
+                rhs_scale=xs[r][:],
+                start=True,
+                stop=False,
+            )
+            nc.tensor.matmul_mx(
+                out=bank[:],
+                lhsT=hq[r][:, P * q : P * q + P].bitcast(FP8X4),
+                lhsT_scale=hs[r][:, P * q : P * q + P],
+                rhs=l_perm[:].bitcast(FP4X4),
+                rhs_scale=l_sc[:],
+                start=False,
+                stop=True,
+            )
+
+        def z_out(r, q):
+            if q == 0:
+                zs[r] = work.tile([P, 4, 512], F32, name="zs", bufs=3, align_bytes=64)
+            k = 4 * r + q
+            nc.scalar.activation(out=zs[r][:, q, :], in_=banks[r, q][:], func=COPY, scale=tau[:, k : k + 1])
+
+        def z_piece(engine, r, lo, hi):
+            engine.tensor_tensor(
+                out=zg[r][:, lo:hi, :].rearrange("p (c i) q -> p c q i", i=4),
+                in0=zs[r][:, :, lo:hi].rearrange("p q (c i) -> p c q i", i=4),
+                in1=xtau[r][:, :, lo:hi].rearrange("p q (c i) -> p c q i", i=4),
+                op=ADD,
+            )
+
+        def quantize_z(r, parts=1):
+            zq[r] = work.tile([P, 512], U32, name="zq", align_bytes=64)
+            zsc[r] = work.tile([P, 512], U8, name="zsc", align_bytes=64)
+            for n in range(parts):
+                w = 512 // parts
+                quantize(zq[r], zsc[r], zg[r], n * w, n * w + w)
+
+        def o_mm(r, t):
+            if r == 0:
+                acc[t] = psum.tile([P, 512], F32, name="acc", tag="acc%d" % t)
+            nc.tensor.matmul_mx(
+                out=acc[t][:],
+                lhsT=zq[r][:, P * t : P * t + P].bitcast(FP8X4),
+                lhsT_scale=zsc[r][:, P * t : P * t + P],
+                rhs=w_sb[:, r, :].bitcast(FP4X4),
+                rhs_scale=w_sc[:, r, :],
+                start=(r == 0),
+                stop=(r == R - 1),
+            )
+
+        out_rows = out.rearrange("(m t) j -> t m j", t=4)
+
+        def finish(t):
+            o_sb = work.tile([P, J], F32, name="o_sb", bufs=4)
+            nc.vector.scalar_tensor_tensor(
+                out=o_sb[:], in0=acc[t][:], scalar=elec[:, t : t + 1], in1=base_sb[:], op0=MULT, op1=ADD
+            )
+            nc.sync.dma_start(out=out_rows[t], in_=o_sb[:])
+
+        def permute_words(dst, src):
+            nc.vector.tensor_copy(
+                out=dst[:].rearrange("p (q m b) -> p m q b", q=4, b=2),
+                in_=src[:].rearrange("p (m q b) -> p m q b", q=4, b=2),
+            )
+
+        def permute_scales(dst, src):
+            nc.vector.tensor_copy(
+                out=dst[:].rearrange("p (q m) -> p m q", q=4), in_=src[:].rearrange("p (m q) -> p m q", q=4)
+            )
+
+        permute_words(a_perm, a_raw)
+        transpose(0)
+        quantize_x(0, 2)
+        permute_scales(a_sc, a_rsc)
+        tau_units = [(r, q) for r in range(R) for q in range(4)]
+        tau_done = 0
+        for i in range(R + 3):
+            order = ORDER
+            if i == 0:
+                order = ORDER0
+            if i == 1:
+                order = ORDER1
+            if i == R:
+                order = ORDER_R
+            if i > R:
+                order = ORDER_T
+            for tok in order.split():
+                c = tok[0]
+                k = int(tok[1]) if len(tok) > 1 else 0
+                if c == "H" and i < R:
+                    h_mm(i, k)
+                if c == "h" and i < R:
+                    h_add(i, k)
+                if c == "Z" and 1 <= i <= R:
+                    z_mm(i - 1, k)
+                    z_out(i - 1, k)
+                if c == "N" and i + 1 < R:
+                    h_mm(i + 1, k)
+                if c == "O" and i >= 3:
+                    o_mm(i - 3, k)
+                    if i == R + 2:
+                        finish(k)
+                if c == "T" and i < 3:
+                    transpose(2 * i + 2 + k)
+                if c == "P" and 2 <= i < R + 2:
+                    if k == 0:
+                        zg[i - 2] = work.tile([P, 512, 4], BF16, name="zg", align_bytes=64)
+                    lo = V_COLS + k * 128
+                    if lo < 512:
+                        z_piece(nc.gpsimd, i - 2, lo, lo + 128)
+                if c == "A" and 2 <= i < R + 2:
+                    w = V_COLS // 4
+                    z_piece(nc.vector, i - 2, k * w, k * w + w)
+                if c == "X" and tau_done < 32:
+                    x_tau(*tau_units[tau_done])
+                    tau_done += 1
+                if c == "Q" and i + 2 < R:
+                    quantize_x(i + 2)
+                if c == "q" and i == 0:
+                    quantize_x(1)
+                if c == "t" and i == 0:
+                    transpose(1)
+                if c == "l" and i == 0:
+                    permute_words(l_perm, l_raw)
+                    permute_scales(l_sc, l_rsc)
+                if c == "u" and i == 0:
+                    nc.vector.tensor_copy(out=tau[:], in_=tau_raw[:].rearrange("p r q -> p (r q)"))
+                if c == "e" and i == 5:
+                    nc.vector.tensor_copy(out=elec[:], in_=elec_raw[:])
+                if c == "G" and i < R:
+                    quantize_h(i)
+                if c == "K" and 2 <= i < R + 2:
+                    quantize_z(i - 2, 2 if i == R + 1 else 1)

@@ -20,13 +20,13 @@ COPY = mybir.ActivationFunctionType.Copy
 P = 128
 X_CHUNKS = ((0,), (1,), (2, 3), (4, 5), (6, 7))
 XT_ON_POOL = ()
-V_COLS = 512
+V_COLS = (512,)*8
 V_T = 2
-ORDER = "h0 H2 Z0 O0 P0 P1 P2 P3 A0 T0 h1 H3 Z1 O1 A1 h2 Z2 O2 N0 A2 T1 h3 Z3 O3 N1 A3 e Q G K X X X X"
-ORDER0 = "H0 H1 h0 u t H2 h1 q H3 T0 h2 N0 h3 N1 T1 X X X X G l Q"
-ORDER1 = "h0 H2 Z0 X T0 h1 H3 Z1 X h2 N0 Z2 X T1 h3 N1 Z3 X Q G"
-ORDER_R = "P0 P1 P2 P3 A0 A1 A2 A3 Z0 Z1 Z2 Z3 O0 O1 O2 O3 K X X X X"
-ORDER_T = "P0 P1 P2 P3 A0 A1 A2 A3 O0 O1 O2 O3 K"
+PW = 128
+FP = ()
+VW = 256
+HB = 2
+XTB = 3
 
 
 def tile_voting_intention_transfer_t2_kernel(
@@ -83,10 +83,15 @@ def tile_voting_intention_transfer_t2_kernel(
                 )
 
         nc.scalar.activation(out=warm[:], in_=warm[:], func=COPY, scale=1.0)
-        load_x(X_CHUNKS[0])
-        nc.sync.dma_start(out=a_raw[:], in_=a_words.rearrange("g p n -> p (g n)"))
-        load_scales(a_rsc, a_scales)
-        load_x(X_CHUNKS[1])
+        for what in "axys":
+            if what == "x":
+                load_x(X_CHUNKS[0])
+            if what == "y":
+                load_x(X_CHUNKS[1])
+            if what == "a":
+                nc.sync.dma_start(out=a_raw[:], in_=a_words.rearrange("g p n -> p (g n)"))
+            if what == "s":
+                load_scales(a_rsc, a_scales)
         nc.sync.dma_start(out=tau_raw[:], in_=turnout.rearrange("(r p q) -> p r q", p=P, q=4))
         load_x(X_CHUNKS[2])
         nc.sync.dma_start(out=l_raw[:], in_=l_words.rearrange("g p n -> p (g n)"))
@@ -135,7 +140,7 @@ def tile_voting_intention_transfer_t2_kernel(
 
         def x_tau(r, q):
             if q == 0:
-                xtau[r] = work.tile([P, 4, 512], F32, name="xtau", bufs=3, align_bytes=64)
+                xtau[r] = work.tile([P, 4, 512], F32, name="xtau", bufs=XTB, align_bytes=64)
             k = 4 * r + q
             if r in XT_ON_POOL:
                 nc.gpsimd.tensor_scalar(
@@ -162,18 +167,18 @@ def tile_voting_intention_transfer_t2_kernel(
 
         def h_add(r, q):
             if q == 0:
-                hg[r] = work.tile([P, 512, 4], BF16, name="hg", align_bytes=64)
+                hg[r] = work.tile([P, 512, 4], BF16, name="hg", bufs=HB, align_bytes=64)
             xn, off = x_view[r]
             nc.vector.tensor_tensor(
-                out=hg[r][:, P * q : P * q + P, :].rearrange("p (c i) t -> p c t i", i=4),
-                in0=banks[r, q][:].rearrange("p t (c i) -> p c t i", i=4),
-                in1=xn[:, :, off : off + 512].rearrange("p t (c i q) -> p q c t i", q=4, i=4)[:, q],
+                out=hg[r][:, P * q : P * q + P, :].rearrange("p (c i) t -> p c t i", i=2),
+                in0=banks[r, q][:].rearrange("p t (c i) -> p c t i", i=2),
+                in1=xn[:, :, off : off + 512].rearrange("p t (c i q) -> p q c t i", q=4, i=2)[:, q],
                 op=ADD,
             )
 
         def quantize_h(r):
-            hq[r] = work.tile([P, 512], U32, name="hq", align_bytes=64)
-            hs[r] = work.tile([P, 512], U8, name="hs", align_bytes=64)
+            hq[r] = work.tile([P, 512], U32, name="hq", bufs=HB, align_bytes=64)
+            hs[r] = work.tile([P, 512], U8, name="hs", bufs=HB, align_bytes=64)
             quantize(hq[r], hs[r], hg[r])
 
         def z_mm(r, q):
@@ -206,11 +211,18 @@ def tile_voting_intention_transfer_t2_kernel(
 
         def z_piece(engine, r, lo, hi):
             engine.tensor_tensor(
-                out=zg[r][:, lo:hi, :].rearrange("p (c i) q -> p c q i", i=4),
-                in0=zs[r][:, :, lo:hi].rearrange("p q (c i) -> p c q i", i=4),
-                in1=xtau[r][:, :, lo:hi].rearrange("p q (c i) -> p c q i", i=4),
+                out=zg[r][:, lo:hi, :].rearrange("p (c i) q -> p c q i", i=2),
+                in0=zs[r][:, :, lo:hi].rearrange("p q (c i) -> p c q i", i=2),
+                in1=xtau[r][:, :, lo:hi].rearrange("p q (c i) -> p c q i", i=2),
                 op=ADD,
             )
+
+        def z_add(r):
+            zg[r] = work.tile([P, 512, 4], BF16, name="zg", align_bytes=64)
+            for lo in range(V_COLS[r], 512, PW):
+                z_piece(nc.gpsimd, r, lo, min(512, lo + PW))
+            for lo in range(0, V_COLS[r], VW):
+                z_piece(nc.vector, r, lo, min(V_COLS[r], lo + VW))
 
         def quantize_z(r, parts=1):
             zq[r] = work.tile([P, 512], U32, name="zq", align_bytes=64)
@@ -236,82 +248,58 @@ def tile_voting_intention_transfer_t2_kernel(
 
         def finish(t):
             o_sb = work.tile([P, J], F32, name="o_sb", bufs=4)
-            nc.vector.scalar_tensor_tensor(
-                out=o_sb[:], in0=acc[t][:], scalar=elec[:, t : t + 1], in1=base_sb[:], op0=MULT, op1=ADD
-            )
+            if t in FP:
+                y_sb = work.tile([P, J], F32, name="y_sb", bufs=2)
+                nc.scalar.activation(out=y_sb[:], in_=acc[t][:], func=COPY, scale=elec[:, t : t + 1])
+                nc.gpsimd.tensor_tensor(out=o_sb[:], in0=y_sb[:], in1=base_sb[:], op=ADD)
+            else:
+                nc.vector.scalar_tensor_tensor(
+                    out=o_sb[:], in0=acc[t][:], scalar=elec[:, t : t + 1], in1=base_sb[:], op0=MULT, op1=ADD
+                )
             nc.sync.dma_start(out=out_rows[t], in_=o_sb[:])
 
-        def permute_words(dst, src):
-            nc.vector.tensor_copy(
-                out=dst[:].rearrange("p (q m b) -> p m q b", q=4, b=2),
-                in_=src[:].rearrange("p (m q b) -> p m q b", q=4, b=2),
+        def permute_words(dst, src, engine=None):
+            (engine or nc.vector).tensor_copy(
+                out=dst[:].rearrange("p (q m b) -> p q m b", q=4, b=2),
+                in_=src[:].rearrange("p (m q b) -> p q m b", q=4, b=2),
             )
 
-        def permute_scales(dst, src):
-            nc.vector.tensor_copy(
-                out=dst[:].rearrange("p (q m) -> p m q", q=4), in_=src[:].rearrange("p (m q) -> p m q", q=4)
+        def permute_scales(dst, src, engine=None):
+            (engine or nc.vector).tensor_copy(
+                out=dst[:].rearrange("p (q m) -> p q m", q=4), in_=src[:].rearrange("p (m q) -> p q m", q=4)
             )
 
+        LP = None
+        LZ, LA, LO = 1, 2, 3
         permute_words(a_perm, a_raw)
         transpose(0)
         quantize_x(0, 2)
         permute_scales(a_sc, a_rsc)
-        tau_units = [(r, q) for r in range(R) for q in range(4)]
-        tau_done = 0
-        for i in range(R + 3):
-            order = ORDER
-            if i == 0:
-                order = ORDER0
-            if i == 1:
-                order = ORDER1
-            if i == R:
-                order = ORDER_R
-            if i > R:
-                order = ORDER_T
-            for tok in order.split():
-                c = tok[0]
-                k = int(tok[1]) if len(tok) > 1 else 0
-                if c == "H" and i < R:
-                    h_mm(i, k)
-                if c == "h" and i < R:
-                    h_add(i, k)
-                if c == "Z" and 1 <= i <= R:
-                    z_mm(i - 1, k)
-                    z_out(i - 1, k)
-                if c == "N" and i + 1 < R:
-                    h_mm(i + 1, k)
-                if c == "O" and i >= 3:
-                    o_mm(i - 3, k)
-                    if i == R + 2:
-                        finish(k)
-                if c == "T" and i < 3:
-                    transpose(2 * i + 2 + k)
-                if c == "P" and 2 <= i < R + 2:
-                    if k == 0:
-                        zg[i - 2] = work.tile([P, 512, 4], BF16, name="zg", align_bytes=64)
-                    lo = V_COLS + k * 128
-                    if lo < 512:
-                        z_piece(nc.gpsimd, i - 2, lo, lo + 128)
-                if c == "A" and 2 <= i < R + 2:
-                    w = V_COLS // 4
-                    z_piece(nc.vector, i - 2, k * w, k * w + w)
-                if c == "X" and tau_done < 32:
-                    x_tau(*tau_units[tau_done])
-                    tau_done += 1
-                if c == "Q" and i + 2 < R:
-                    quantize_x(i + 2)
-                if c == "q" and i == 0:
-                    quantize_x(1)
-                if c == "t" and i == 0:
-                    transpose(1)
-                if c == "l" and i == 0:
-                    permute_words(l_perm, l_raw)
-                    permute_scales(l_sc, l_rsc)
-                if c == "u" and i == 0:
-                    nc.vector.tensor_copy(out=tau[:], in_=tau_raw[:].rearrange("p r q -> p (r q)"))
-                if c == "e" and i == 5:
-                    nc.vector.tensor_copy(out=elec[:], in_=elec_raw[:])
-                if c == "G" and i < R:
-                    quantize_h(i)
-                if c == "K" and 2 <= i < R + 2:
-                    quantize_z(i - 2, 2 if i == R + 1 else 1)
+        nc.vector.tensor_copy(out=tau[:], in_=tau_raw[:].rearrange("p r q -> p (r q)"))
+        for r in range(1, R):
+            transpose(r)
+        permute_words(l_perm, l_raw, LP)
+        permute_scales(l_sc, l_rsc, LP)
+        for i in range(R + LO):
+            if i < R:
+                if i + 1 < R:
+                    quantize_x(i + 1)
+                for q in range(4):
+                    h_mm(i, q)
+                    h_add(i, q)
+                quantize_h(i)
+            if LZ <= i < R + LZ:
+                for q in range(4):
+                    x_tau(i - LZ, q)
+                    z_mm(i - LZ, q)
+                    z_out(i - LZ, q)
+            if LA <= i < R + LA:
+                z_add(i - LA)
+                quantize_z(i - LA, 2 if i - LA == R - 1 else 1)
+            if i == 5:
+                nc.vector.tensor_copy(out=elec[:], in_=elec_raw[:])
+            if i >= LO:
+                for t in range(4):
+                    o_mm(i - LO, t)
+                    if i == R + LO - 1:
+                        finish(t)

@@ -19,24 +19,25 @@ COPY = mybir.ActivationFunctionType.Copy
 
 P = 128
 X_CHUNKS = ((0,), (1,), (2, 3), (4, 5), (6, 7))
-XT_ON_POOL = ()
-V_COLS = (512,)*8
-V_T = 2
-PW = 128
-FP = ()
-VW = 256
-HB = 2
-XTB = 3
+XTAU = {(0, q): 'G' for q in range(4)}
+COPY_T = ()
+PIECES = [(('V', 0, 128), ('V', 128, 256), ('G', 256, 384), ('G', 384, 512))] * 6 + [(('V', 0, 256), ('V', 256, 512), ('G', 512, 512), ('G', 512, 512))[:2]] * 2
+FIN = ()
+HPOOL = ()
+LOADS = "Gi Gm Qx0 Qas Qa Qx1 Qt Qe Qx2 Ql Qls Qx3 Qx4 Qw Qws Qb"
+STEPS = ('a T b T Q Q T c H0 H1 T X h0 X h1 H2 X h2 X Q H3 h3 G X X T T T N1 N0', 'X h1 h0 T H2 m l X Q h2 H3 T T Z1 h3 Z0 N1 Z2 Z3 N0 G Q', 'h1 X T Z3 A3 Z0 h0 H3 A0 h3 H2 h2 X Z1 Q Z2 A2 N1 A1 N0 G', 'X h1 T T Z0 h0 A3 Z2 H3 H2 Q A0 O1 h3 h2 X Z3 O0 A2 A1 Z1 O3 O2 G J T N1 X X N0', 'X h1 T T Z0 h0 A3 Z2 H3 H2 Q A0 O1 h3 h2 X Z3 O0 A2 A1 Z1 O3 O2 G J T N1 X X N0', 'X h1 T T Z0 h0 A3 Z2 H3 H2 Q A0 O1 h3 h2 X Z3 O0 A2 A1 Z1 O3 O2 G J T N1 X X N0', 'X h1 T T Z0 h0 A3 Z2 H3 H2 Q A0 O1 h3 h2 X Z3 O0 A2 A1 Z1 O3 O2 G J T N1 X X N0', 'Z3 Z0 O2 A1 A3 Q A2 J X h1 h0 X Z2 H2 h2 H3 Z1 X X T h3 O0 A0 O1 X T T G T X X O3', 'Z3 Z0 A1 Z2 Z1 O0 y3 O3 A0 y0 O1 y1 J y2 y4 y7 y6 y5 O2 K', 'A0 T T O1 k0 A1 k1 T O2 O0 k2 k3 O3', 'O2 O1 O0 O3', 'T O0 F0 O2 O1 O3 F2 F1 F3')
 
 
 def tile_voting_intention_transfer_t2_kernel(
     tc, x, a_words, a_scales, l_words, l_scales, turnout, w_words, w_scales, electorate, base, out
 ):
     nc = tc.nc
+    engines = {"V": nc.vector, "S": nc.scalar, "G": nc.gpsimd, "Q": nc.sync}
     with ExitStack() as ctx:
         keep = ctx.enter_context(tc.tile_pool(name="keep", bufs=1))
         work = ctx.enter_context(tc.tile_pool(name="work", bufs=2))
         psum = ctx.enter_context(tc.psum_pool(name="psum", bufs=1))
+        ctx.enter_context(tc.manual_schedule())
 
         a_rsc = keep.tile([P, 512], U8, align_bytes=64)
         l_rsc = keep.tile([P, 512], U8, align_bytes=64)
@@ -48,108 +49,123 @@ def tile_voting_intention_transfer_t2_kernel(
         l_perm = keep.tile([P, 1024], U8, align_bytes=64)
         w_sb = keep.tile([P, R, 1024], U8, align_bytes=64)
         w_sc = keep.tile([P, R, 512], U8, align_bytes=64)
-        tau_raw = keep.tile([P, R, 4], BF16)
-        tau = keep.tile([P, R * 4], F32)
-        elec_raw = keep.tile([P, 4], BF16)
-        elec = keep.tile([P, 4], F32)
+        vec_rows = keep.tile([P, 512], BF16, align_bytes=64)
+        vec = keep.tile([P, (R + 1) * 4], F32)
         base_sb = keep.tile([P, J], BF16)
         ident = keep.tile([P, P], F32)
         warm = keep.tile([P, 1], F32)
 
+        nc.vector.memset(vec_rows[:].bitcast(F32), 0.0)
         nc.vector.memset(a_rsc[:].bitcast(I32), 0)
         nc.vector.memset(l_rsc[:].bitcast(I32), 0)
         nc.vector.memset(warm[:], 0.0)
-        make_identity(nc, ident[:])
-        nc.gpsimd.memset(w_sc[:].rearrange("p g n -> p (g n)").bitcast(I32), 0)
+        nc.scalar.activation(out=warm[:], in_=warm[:], func=COPY, scale=1.0)
 
         x_view = {}
+        a_src = a_words.rearrange("g p n -> p (g n)")
+        l_src = l_words.rearrange("g p n -> p (g n)")
 
-        def load_x(chunk):
+        def load_x(queue, n):
+            chunk = X_CHUNKS[n]
             width = 512 * len(chunk)
             xn = keep.tile([P, 4, width], BF16, name="x_rows%d" % chunk[0], align_bytes=64)
             rows = x[:, 512 * chunk[0] : 512 * chunk[0] + width].rearrange("(p t) c -> p t c", t=4)
-            if chunk[0] == 0:
+            if n == 0:
                 for h in range(2):
-                    nc.sync.dma_start(out=xn[:, 2 * h : 2 * h + 2, :], in_=rows[:, 2 * h : 2 * h + 2, :])
+                    queue.dma_start(out=xn[:, 2 * h : 2 * h + 2, :], in_=rows[:, 2 * h : 2 * h + 2, :])
             else:
-                nc.sync.dma_start(out=xn[:], in_=rows)
+                queue.dma_start(out=xn[:], in_=rows)
             for n, r in enumerate(chunk):
                 x_view[r] = (xn, 512 * n)
 
-        def load_scales(dst, s):
+        def load_scales(queue, dst, s):
             for qd in range(4):
-                nc.sync.dma_start(
+                queue.dma_start(
                     out=dst[32 * qd : 32 * qd + 4, :].bitcast(I32), in_=s[0, 4 * qd : 4 * qd + 4, :].bitcast(I32)
                 )
 
-        nc.scalar.activation(out=warm[:], in_=warm[:], func=COPY, scale=1.0)
-        for what in "axys":
-            if what == "x":
-                load_x(X_CHUNKS[0])
-            if what == "y":
-                load_x(X_CHUNKS[1])
-            if what == "a":
-                nc.sync.dma_start(out=a_raw[:], in_=a_words.rearrange("g p n -> p (g n)"))
-            if what == "s":
-                load_scales(a_rsc, a_scales)
-        nc.sync.dma_start(out=tau_raw[:], in_=turnout.rearrange("(r p q) -> p r q", p=P, q=4))
-        load_x(X_CHUNKS[2])
-        nc.sync.dma_start(out=l_raw[:], in_=l_words.rearrange("g p n -> p (g n)"))
-        load_scales(l_rsc, l_scales)
-        for chunk in X_CHUNKS[3:]:
-            load_x(chunk)
-        nc.sync.dma_start(out=w_sb[:], in_=w_words.rearrange("g p n -> p g n"))
-        for qd in range(4):
-            nc.sync.dma_start(
-                out=w_sc[32 * qd : 32 * qd + 4, :, :].bitcast(I32),
-                in_=w_scales[:, 4 * qd : 4 * qd + 4, :].bitcast(I32).rearrange("g q n -> q g n"),
-            )
-        nc.sync.dma_start(out=elec_raw[:], in_=electorate.rearrange("(m t) -> m t", t=4))
-        nc.sync.dma_start(out=base_sb[:], in_=base.partition_broadcast(P))
+        for word in LOADS.split():
+            queue, what = engines[word[0]], word[1:]
+            if what == "i":
+                make_identity(nc, ident[:])
+            elif what == "m":
+                nc.gpsimd.memset(w_sc[:].rearrange("p g n -> p (g n)").bitcast(I32), 0)
+            elif what == "a":
+                queue.dma_start(out=a_raw[:], in_=a_src)
+            elif what == "l":
+                queue.dma_start(out=l_raw[:], in_=l_src)
+            elif what == "as":
+                load_scales(queue, a_rsc, a_scales)
+            elif what == "ls":
+                load_scales(queue, l_rsc, l_scales)
+            elif what == "t":
+                queue.dma_start(out=vec_rows[0:R, :], in_=turnout.rearrange("(r c) -> r c", r=R))
+            elif what == "w":
+                queue.dma_start(out=w_sb[:], in_=w_words.rearrange("g p n -> p g n"))
+            elif what == "ws":
+                for qd in range(4):
+                    queue.dma_start(
+                        out=w_sc[32 * qd : 32 * qd + 4, :, :].bitcast(I32),
+                        in_=w_scales[:, 4 * qd : 4 * qd + 4, :].bitcast(I32).rearrange("g q n -> q g n"),
+                    )
+            elif what == "e":
+                queue.dma_start(out=vec_rows[R : R + 1, :], in_=electorate.rearrange("(r c) -> r c", r=1))
+            elif what == "b":
+                queue.dma_start(out=base_sb[:], in_=base.partition_broadcast(P))
+            else:
+                load_x(queue, int(what[1:]))
 
         xt, xq, xs, xtau, hg, hq, hs, zs, zg, zq, zsc, acc = {}, {}, {}, {}, {}, {}, {}, {}, {}, {}, {}, {}
+        banks, zbanks = {}, {}
 
-        def transpose(r):
+        def transpose(r, b):
             xn, off = x_view[r]
-            xt[r] = keep.tile([P, 512, 4], BF16, name="xt%d" % r, align_bytes=64)
+            if b == 0:
+                xt[r] = keep.tile([P, 512, 4], BF16, name="xt%d" % r, align_bytes=64)
             words = xn[:].bitcast(F32)
-            for b in range(2):
-                bank = psum.tile([P, 2, 2, P], F32, name="tp", tag="acc%d" % (2 * (r % 2) + b))
-                for t in range(2):
-                    for u in range(2):
-                        lo = off // 2
-                        nc.tensor.transpose(bank[:, t, u, :], words[:, 2 * b + t, lo + u : lo + 256 : 2], ident[:])
-                (nc.vector.tensor_copy if (r < V_T and b == 1) else nc.scalar.copy)(
-                    out=xt[r][:].bitcast(F32)[:, 256 * b : 256 * b + 256, :].rearrange("p (t m) u -> p t m u", t=2),
-                    in_=bank[:].rearrange("p t u m -> p t m u"),
-                )
+            bank = psum.tile([P, 2, 2, P], F32, name="tp", tag="acc%d" % (2 * (r % 2) + b))
+            for t in range(2):
+                for u in range(2):
+                    lo = off // 2
+                    nc.tensor.transpose(bank[:, t, u, :], words[:, 2 * b + t, lo + u : lo + 256 : 2], ident[:])
+            (nc.vector.tensor_copy if (r, b) in COPY_T else nc.scalar.copy)(
+                out=xt[r][:].bitcast(F32)[:, 256 * b : 256 * b + 256, :].rearrange("p (t m) u -> p t m u", t=2),
+                in_=bank[:].rearrange("p t u m -> p t m u"),
+            )
 
-        def quantize(codes, scales, grouped, lo=0, hi=512):
+        def vectors():
+            bank = psum.tile([P, 2, P], F32, name="tv", tag="acc3")
+            for u in range(2):
+                nc.tensor.transpose(bank[:, u, :], vec_rows[:].bitcast(F32)[:, u::2], ident[:])
+            nc.vector.tensor_copy(
+                out=vec[:].rearrange("p (r u e) -> p r u e", u=2, e=2),
+                in_=bank[:].bitcast(BF16)[:, :, 0 : 2 * (R + 1)].rearrange("p u (r e) -> p r u e", e=2),
+            )
+
+        def quantize(codes, scales, grouped, lo, hi):
             nc.vector.quantize_mx(
                 out=codes[:, lo:hi].bitcast(FP8X4),
                 scales=scales[:, lo:hi],
                 in_=grouped[:, lo:hi, :].rearrange("p e t -> p (e t)"),
             )
 
-        def quantize_x(r, parts=1):
-            xq[r] = keep.tile([P, 512], U32, name="xq%d" % r, align_bytes=64)
-            xs[r] = keep.tile([P, 512], U8, name="xs%d" % r, align_bytes=64)
-            for n in range(parts):
-                w = 512 // parts
-                quantize(xq[r], xs[r], xt[r], n * w, n * w + w)
+        def quantize_x(r, lo, hi):
+            if lo == 0:
+                xq[r] = keep.tile([P, 512], U32, name="xq%d" % r, align_bytes=64)
+                xs[r] = keep.tile([P, 512], U8, name="xs%d" % r, align_bytes=64)
+            quantize(xq[r], xs[r], xt[r], lo, hi)
 
         def x_tau(r, q):
-            if q == 0:
-                xtau[r] = work.tile([P, 4, 512], F32, name="xtau", bufs=XTB, align_bytes=64)
-            k = 4 * r + q
-            if r in XT_ON_POOL:
-                nc.gpsimd.tensor_scalar(
-                    out=xtau[r][:, q, :], in0=xt[r][:, :, q], scalar1=tau[:, k : k + 1], scalar2=0.0, op0=MULT, op1=ADD
-                )
+            if r not in xtau:
+                xtau[r] = work.tile([P, 4, 512], F32, name="xtau", bufs=3, align_bytes=64)
+            factor = vec[:, 4 * r + q : 4 * r + q + 1]
+            engine = XTAU.get((r, q), "S")
+            if engine == "S":
+                nc.scalar.activation(out=xtau[r][:, q, :], in_=xt[r][:, :, q], func=COPY, scale=factor)
             else:
-                nc.scalar.activation(out=xtau[r][:, q, :], in_=xt[r][:, :, q], func=COPY, scale=tau[:, k : k + 1])
-
-        banks = {}
+                engines[engine].tensor_scalar(
+                    out=xtau[r][:, q, :], in0=xt[r][:, :, q], scalar1=factor, scalar2=0.0, op0=MULT, op1=ADD
+                )
 
         def h_mm(r, q):
             bank = psum.tile([P, 4, P], F32, name="hbank", tag="h", bufs=2)
@@ -166,24 +182,30 @@ def tile_voting_intention_transfer_t2_kernel(
                 )
 
         def h_add(r, q):
-            if q == 0:
-                hg[r] = work.tile([P, 512, 4], BF16, name="hg", bufs=HB, align_bytes=64)
+            if r not in hg:
+                hg[r] = work.tile([P, 512, 4], BF16, name="hg", bufs=2, align_bytes=64)
             xn, off = x_view[r]
-            nc.vector.tensor_tensor(
+            source, engine = banks[r, q], nc.vector
+            if (r, q) in HPOOL:
+                source, engine = work.tile([P, 4, P], F32, name="hs32", align_bytes=64), nc.gpsimd
+                nc.scalar.copy(out=source[:], in_=banks[r, q][:])
+            engine.tensor_tensor(
                 out=hg[r][:, P * q : P * q + P, :].rearrange("p (c i) t -> p c t i", i=2),
-                in0=banks[r, q][:].rearrange("p t (c i) -> p c t i", i=2),
+                in0=source[:].rearrange("p t (c i) -> p c t i", i=2),
                 in1=xn[:, :, off : off + 512].rearrange("p t (c i q) -> p q c t i", q=4, i=2)[:, q],
                 op=ADD,
             )
 
         def quantize_h(r):
-            hq[r] = work.tile([P, 512], U32, name="hq", bufs=HB, align_bytes=64)
-            hs[r] = work.tile([P, 512], U8, name="hs", bufs=HB, align_bytes=64)
-            quantize(hq[r], hs[r], hg[r])
+            hq[r] = work.tile([P, 512], U32, name="hq", bufs=2, align_bytes=64)
+            hs[r] = work.tile([P, 512], U8, name="hs", bufs=2, align_bytes=64)
+            quantize(hq[r], hs[r], hg[r], 0, 512)
 
         def z_mm(r, q):
-            bank = psum.tile([P, 512], F32, name="zbank", tag="z", bufs=2)
-            banks[r, q] = bank
+            bank = psum.tile([P, 512], F32, name="zbank", tag="h" if 1 and r == R - 1 and q >= 2 else "z", bufs=2)
+            zbanks[r, q] = bank
+            if r not in zs:
+                zs[r] = work.tile([P, 4, 512], F32, name="zs", bufs=3, align_bytes=64)
             nc.tensor.matmul_mx(
                 out=bank[:],
                 lhsT=a_perm[:, 256 * q : 256 * q + 256].bitcast(FP4X4),
@@ -202,37 +224,36 @@ def tile_voting_intention_transfer_t2_kernel(
                 start=False,
                 stop=True,
             )
+            if not (1 and r == R - 1):
+                z_out(r, q, 0, 512)
 
-        def z_out(r, q):
-            if q == 0:
-                zs[r] = work.tile([P, 4, 512], F32, name="zs", bufs=3, align_bytes=64)
+        def z_out(r, q, lo, hi):
             k = 4 * r + q
-            nc.scalar.activation(out=zs[r][:, q, :], in_=banks[r, q][:], func=COPY, scale=tau[:, k : k + 1])
+            nc.scalar.activation(
+                out=zs[r][:, q, lo:hi], in_=zbanks[r, q][:, lo:hi], func=COPY, scale=vec[:, k : k + 1]
+            )
 
-        def z_piece(engine, r, lo, hi):
-            engine.tensor_tensor(
+        def z_piece(r, n):
+            if n >= len(PIECES[r]):
+                return
+            if r not in zg:
+                zg[r] = work.tile([P, 512, 4], BF16, name="zg", align_bytes=64)
+            name, lo, hi = PIECES[r][n]
+            engines[name].tensor_tensor(
                 out=zg[r][:, lo:hi, :].rearrange("p (c i) q -> p c q i", i=2),
                 in0=zs[r][:, :, lo:hi].rearrange("p q (c i) -> p c q i", i=2),
                 in1=xtau[r][:, :, lo:hi].rearrange("p q (c i) -> p c q i", i=2),
                 op=ADD,
             )
 
-        def z_add(r):
-            zg[r] = work.tile([P, 512, 4], BF16, name="zg", align_bytes=64)
-            for lo in range(V_COLS[r], 512, PW):
-                z_piece(nc.gpsimd, r, lo, min(512, lo + PW))
-            for lo in range(0, V_COLS[r], VW):
-                z_piece(nc.vector, r, lo, min(V_COLS[r], lo + VW))
-
-        def quantize_z(r, parts=1):
-            zq[r] = work.tile([P, 512], U32, name="zq", align_bytes=64)
-            zsc[r] = work.tile([P, 512], U8, name="zsc", align_bytes=64)
-            for n in range(parts):
-                w = 512 // parts
-                quantize(zq[r], zsc[r], zg[r], n * w, n * w + w)
+        def quantize_z(r, lo, hi):
+            if r not in zq:
+                zq[r] = work.tile([P, 512], U32, name="zq", bufs=3, align_bytes=64)
+                zsc[r] = work.tile([P, 512], U8, name="zsc", bufs=3, align_bytes=64)
+            quantize(zq[r], zsc[r], zg[r], lo, hi)
 
         def o_mm(r, t):
-            if r == 0:
+            if t not in acc:
                 acc[t] = psum.tile([P, 512], F32, name="acc", tag="acc%d" % t)
             nc.tensor.matmul_mx(
                 out=acc[t][:],
@@ -248,58 +269,81 @@ def tile_voting_intention_transfer_t2_kernel(
 
         def finish(t):
             o_sb = work.tile([P, J], F32, name="o_sb", bufs=4)
-            if t in FP:
+            if t in FIN:
                 y_sb = work.tile([P, J], F32, name="y_sb", bufs=2)
-                nc.scalar.activation(out=y_sb[:], in_=acc[t][:], func=COPY, scale=elec[:, t : t + 1])
+                nc.scalar.activation(out=y_sb[:], in_=acc[t][:], func=COPY, scale=vec[:, 4 * R + t : 4 * R + t + 1])
                 nc.gpsimd.tensor_tensor(out=o_sb[:], in0=y_sb[:], in1=base_sb[:], op=ADD)
             else:
                 nc.vector.scalar_tensor_tensor(
-                    out=o_sb[:], in0=acc[t][:], scalar=elec[:, t : t + 1], in1=base_sb[:], op0=MULT, op1=ADD
+                    out=o_sb[:], in0=acc[t][:], scalar=vec[:, 4 * R + t : 4 * R + t + 1], in1=base_sb[:], op0=MULT, op1=ADD
                 )
             nc.sync.dma_start(out=out_rows[t], in_=o_sb[:])
 
-        def permute_words(dst, src, engine=None):
-            (engine or nc.vector).tensor_copy(
+        def permute_words(dst, src):
+            nc.vector.tensor_copy(
                 out=dst[:].rearrange("p (q m b) -> p q m b", q=4, b=2),
                 in_=src[:].rearrange("p (m q b) -> p q m b", q=4, b=2),
             )
 
-        def permute_scales(dst, src, engine=None):
-            (engine or nc.vector).tensor_copy(
+        def permute_scales(dst, src):
+            nc.vector.tensor_copy(
                 out=dst[:].rearrange("p (q m) -> p q m", q=4), in_=src[:].rearrange("p (m q) -> p q m", q=4)
             )
 
-        LP = None
-        LZ, LA, LO = 1, 2, 3
-        permute_words(a_perm, a_raw)
-        transpose(0)
-        quantize_x(0, 2)
-        permute_scales(a_sc, a_rsc)
-        nc.vector.tensor_copy(out=tau[:], in_=tau_raw[:].rearrange("p r q -> p (r q)"))
-        for r in range(1, R):
-            transpose(r)
-        permute_words(l_perm, l_raw, LP)
-        permute_scales(l_sc, l_rsc, LP)
-        for i in range(R + LO):
-            if i < R:
+        counters = {"T": 0, "Q": 0, "X": 0}
+        queues = {
+            "T": [(r, b) for r in range(R) for b in range(2)],
+            "Q": [(0, 0, 256), (0, 256, 512)] + [(r, 0, 512) for r in range(1, R)],
+            "X": [(r, q) for r in range(R) for q in range(4)],
+        }
+
+        def run(c, k, i):
+            if c in counters:
+                n = counters[c]
+                if n < len(queues[c]):
+                    counters[c] = n + 1
+                    {"T": transpose, "Q": quantize_x, "X": x_tau}[c](*queues[c][n])
+            elif c == "H":
+                h_mm(i, k)
+            elif c == "N":
                 if i + 1 < R:
-                    quantize_x(i + 1)
-                for q in range(4):
-                    h_mm(i, q)
-                    h_add(i, q)
+                    h_mm(i + 1, k)
+            elif c == "h":
+                h_add(i, k)
+            elif c == "G":
                 quantize_h(i)
-            if LZ <= i < R + LZ:
-                for q in range(4):
-                    x_tau(i - LZ, q)
-                    z_mm(i - LZ, q)
-                    z_out(i - LZ, q)
-            if LA <= i < R + LA:
-                z_add(i - LA)
-                quantize_z(i - LA, 2 if i - LA == R - 1 else 1)
-            if i == 5:
-                nc.vector.tensor_copy(out=elec[:], in_=elec_raw[:])
-            if i >= LO:
-                for t in range(4):
-                    o_mm(i - LO, t)
-                    if i == R + LO - 1:
-                        finish(t)
+            elif c == "Z":
+                z_mm(i - 1, k)
+            elif c == "A":
+                z_piece(i - 2, k)
+            elif c == "B":
+                if i > 2:
+                    z_piece(i - 3, k)
+            elif c == "K":
+                quantize_z(i - 2, 0, 512)
+            elif c == "J":
+                if i > 2:
+                    quantize_z(i - 3, 0, 512)
+            elif c == "k":
+                quantize_z(i - 2, P * k, P * k + P)
+            elif c == "O":
+                if i > 3:
+                    o_mm(i - 4, k)
+            elif c == "F":
+                finish(k)
+            elif c == "a":
+                permute_words(a_perm, a_raw)
+            elif c == "b":
+                permute_scales(a_sc, a_rsc)
+            elif c == "l":
+                permute_words(l_perm, l_raw)
+            elif c == "m":
+                permute_scales(l_sc, l_rsc)
+            elif c == "y":
+                z_out(R - 1, k % 4, 256 * (k // 4), 256 * (k // 4) + 256)
+            elif c == "c":
+                vectors()
+
+        for i in range(R + 4):
+            for word in STEPS[i].split():
+                run(word[0], int(word[1:] or 0), i)

@@ -18,14 +18,14 @@ MULT = mybir.AluOpType.mult
 COPY = mybir.ActivationFunctionType.Copy
 
 P = 128
-X_CHUNKS = ((0,), (1,), (2, 3), (4, 5), (6, 7))
+X_CHUNKS = ((0,), (1,), (2,), (3,), (4, 5), (6, 7))
 XTAU = {(0, q): 'G' for q in range(4)}
 COPY_T = ()
 PIECES = [(('V', 0, 128), ('V', 128, 256), ('G', 256, 384), ('G', 384, 512))] * 6 + [(('V', 0, 256), ('V', 256, 512), ('G', 512, 512), ('G', 512, 512))[:2]] * 2
 FIN = ()
 HPOOL = ()
-LOADS = "Gi Gm Qx0 Qas Qa Qx1 Qt Qe Qx2 Ql Qls Qx3 Qx4 Qw Qws Qb"
-STEPS = ('a T b T Q Q T c H0 H1 T X h0 X h1 H2 X h2 X Q H3 h3 G X X T T T N1 N0', 'X h1 h0 T H2 m l X Q h2 H3 T T Z1 h3 Z0 N1 Z2 Z3 N0 G Q', 'h1 X T Z3 A3 Z0 h0 H3 A0 h3 H2 h2 X Z1 Q Z2 A2 N1 A1 N0 G', 'X h1 T T Z0 h0 A3 Z2 H3 H2 Q A0 O1 h3 h2 X Z3 O0 A2 A1 Z1 O3 O2 G J T N1 X X N0', 'X h1 T T Z0 h0 A3 Z2 H3 H2 Q A0 O1 h3 h2 X Z3 O0 A2 A1 Z1 O3 O2 G J T N1 X X N0', 'X h1 T T Z0 h0 A3 Z2 H3 H2 Q A0 O1 h3 h2 X Z3 O0 A2 A1 Z1 O3 O2 G J T N1 X X N0', 'X h1 T T Z0 h0 A3 Z2 H3 H2 Q A0 O1 h3 h2 X Z3 O0 A2 A1 Z1 O3 O2 G J T N1 X X N0', 'Z3 Z0 O2 A1 A3 Q A2 J X h1 h0 X Z2 H2 h2 H3 Z1 X X T h3 O0 A0 O1 X T T G T X X O3', 'Z3 Z0 A1 Z2 Z1 O0 y3 O3 A0 y0 O1 y1 J y2 y4 y7 y6 y5 O2 K', 'A0 T T O1 k0 A1 k1 T O2 O0 k2 k3 O3', 'O2 O1 O0 O3', 'T O0 F0 O2 O1 O3 F2 F1 F3')
+LOADS = "Gi Gm Qx0 Qas Qa Qx1 Qt Qe Qx2 Ql Qls Qx3 Qx4 Qx5 Qw Qws Qb"
+STEPS = ('T Q T T a b Q H1 H3 h1 h3 H2 h2 T H0 h0 c X T T Q X N0 X N1 l X X G', 'H3 X X X h0 m h1 Q T h3 T Z2 Z1 H2 Z3 h2 N1 Z0 N0 G', 'A2 H3 X X Z0 T T Q A1 h1 Z1 h3 H2 h0 A3 Z2 h2 Z3 T T N1 Q G A0 N0', 'A0 X h1 X X h0 A3 H2 Z0 h2 H3 h3 Z2 Z3 Z1 T A1 T J N1 X N0 O0 Q A2 G O1', 'A0 X h1 X X h0 A3 H2 Z0 h2 H3 h3 Z2 Z3 Z1 T A1 T J N1 X N0 O0 Q A2 G O1', 'A0 X h1 X X h0 A3 H2 Z0 h2 H3 h3 Z2 Z3 Z1 T A1 T J N1 X N0 O0 Q A2 G O1', 'A0 X h1 X X h0 A3 H2 Z0 h2 H3 h3 Z2 Z3 Z1 T A1 T J N1 X N0 O0 Q A2 G O1', 'A1 X h1 Z3 H2 X O0 Z0 A2 h2 H3 h0 Z2 Z1 h3 J G X O1 A0 T A3', 'T R2 T R3 O1 A1 X Z1 X Z2 y5 Z3 y6 X y7 Z0 y4 y3 T y1 y0 A0 R2 R3 O0 J K y2', 'A1 A0 R3 k0 k2 k3 k1 R2 O1 R3 O0 R2', 'T Q R3 T R2 R2 O0 R3 T X O1', 'O0 T R2 O1 R3 F0 R2 R3 F1 F3 F2')
 
 
 def tile_voting_intention_transfer_t2_kernel(
@@ -123,7 +123,7 @@ def tile_voting_intention_transfer_t2_kernel(
             if b == 0:
                 xt[r] = keep.tile([P, 512, 4], BF16, name="xt%d" % r, align_bytes=64)
             words = xn[:].bitcast(F32)
-            bank = psum.tile([P, 2, 2, P], F32, name="tp", tag="acc%d" % (2 * (r % 2) + b))
+            bank = psum.tile([P, 2, 2, P], F32, name="tp", tag="acc%d" % (b))
             for t in range(2):
                 for u in range(2):
                     lo = off // 2
@@ -134,7 +134,7 @@ def tile_voting_intention_transfer_t2_kernel(
             )
 
         def vectors():
-            bank = psum.tile([P, 2, P], F32, name="tv", tag="acc3")
+            bank = psum.tile([P, 2, P], F32, name="tv", tag="z", bufs=3)
             for u in range(2):
                 nc.tensor.transpose(bank[:, u, :], vec_rows[:].bitcast(F32)[:, u::2], ident[:])
             nc.vector.tensor_copy(
@@ -168,7 +168,7 @@ def tile_voting_intention_transfer_t2_kernel(
                 )
 
         def h_mm(r, q):
-            bank = psum.tile([P, 4, P], F32, name="hbank", tag="h", bufs=2)
+            bank = psum.tile([P, 4, P], F32, name="hbank", tag="h", bufs=3)
             banks[r, q] = bank
             for t in range(4):
                 nc.tensor.matmul_mx(
@@ -202,7 +202,7 @@ def tile_voting_intention_transfer_t2_kernel(
             quantize(hq[r], hs[r], hg[r], 0, 512)
 
         def z_mm(r, q):
-            bank = psum.tile([P, 512], F32, name="zbank", tag="h" if 1 and r == R - 1 and q >= 2 else "z", bufs=2)
+            bank = psum.tile([P, 512], F32, name="zbank", tag="h" if 1 and r == R - 1 and q >= 3 else "z", bufs=3)
             zbanks[r, q] = bank
             if r not in zs:
                 zs[r] = work.tile([P, 4, 512], F32, name="zs", bufs=3, align_bytes=64)
@@ -240,21 +240,21 @@ def tile_voting_intention_transfer_t2_kernel(
                 zg[r] = work.tile([P, 512, 4], BF16, name="zg", align_bytes=64)
             name, lo, hi = PIECES[r][n]
             engines[name].tensor_tensor(
-                out=zg[r][:, lo:hi, :].rearrange("p (c i) q -> p c q i", i=2),
-                in0=zs[r][:, :, lo:hi].rearrange("p q (c i) -> p c q i", i=2),
-                in1=xtau[r][:, :, lo:hi].rearrange("p q (c i) -> p c q i", i=2),
+                out=zg[r][:, lo:hi, :].rearrange("p (c i) q -> p c q i", i=4),
+                in0=zs[r][:, :, lo:hi].rearrange("p q (c i) -> p c q i", i=4),
+                in1=xtau[r][:, :, lo:hi].rearrange("p q (c i) -> p c q i", i=4),
                 op=ADD,
             )
 
         def quantize_z(r, lo, hi):
             if r not in zq:
-                zq[r] = work.tile([P, 512], U32, name="zq", bufs=3, align_bytes=64)
-                zsc[r] = work.tile([P, 512], U8, name="zsc", bufs=3, align_bytes=64)
+                zq[r] = work.tile([P, 512], U32, name="zq", bufs=8, align_bytes=64)
+                zsc[r] = work.tile([P, 512], U8, name="zsc", bufs=8, align_bytes=64)
             quantize(zq[r], zsc[r], zg[r], lo, hi)
 
         def o_mm(r, t):
             if t not in acc:
-                acc[t] = psum.tile([P, 512], F32, name="acc", tag="acc%d" % t)
+                acc[t] = psum.tile([P, 512], F32, name="acc", tag="acc%d" % t if t < 2 else "h", bufs=1 if t < 2 else 3)
             nc.tensor.matmul_mx(
                 out=acc[t][:],
                 lhsT=zq[r][:, P * t : P * t + P].bitcast(FP8X4),
@@ -290,6 +290,7 @@ def tile_voting_intention_transfer_t2_kernel(
                 out=dst[:].rearrange("p (q m) -> p q m", q=4), in_=src[:].rearrange("p (m q) -> p q m", q=4)
             )
 
+        late = {2: 0, 3: 0}
         counters = {"T": 0, "Q": 0, "X": 0}
         queues = {
             "T": [(r, b) for r in range(R) for b in range(2)],
@@ -329,6 +330,9 @@ def tile_voting_intention_transfer_t2_kernel(
             elif c == "O":
                 if i > 3:
                     o_mm(i - 4, k)
+            elif c == "R":
+                o_mm(late[k], k)
+                late[k] += 1
             elif c == "F":
                 finish(k)
             elif c == "a":

from contextlib import ExitStack

import concourse.mybir as mybir
from concourse.masks import make_identity

D, R, C, J = 512, 8, 512, 512
FLOPS = 3 * 2 * 512 * 512 * 4096

F32 = mybir.dt.float32
BF16 = mybir.dt.bfloat16
I32 = mybir.dt.int32
U32 = mybir.dt.uint32
U8 = mybir.dt.uint8
FP8X4 = mybir.dt.float8_e4m3fn_x4
FP4X4 = mybir.dt.float4_e2m1fn_x4
ADD = mybir.AluOpType.add
MULT = mybir.AluOpType.mult
COPY = mybir.ActivationFunctionType.Copy

P = 128
X_CHUNKS = ((0,), (1,), (2,), (3,), (4, 5), (6, 7))
XTAU = {(0, q): 'G' for q in range(4)}
COPY_T = ()
PIECES = [(('V', 0, 128), ('V', 128, 256), ('G', 256, 384), ('G', 384, 512))] * 6 + [(('V', 0, 256), ('V', 256, 512), ('G', 512, 512), ('G', 512, 512))[:2]] * 2
FIN = ()
HPOOL = ()
LOADS = "Gi Gm Qx0 Qas Qa Qx1 Qt Qe Qx2 Ql Qls Qx3 Qx4 Qx5 Qw Qws Qb"
STEPS = ('T Q T T a b Q H1 H3 h1 h3 H2 h2 T H0 h0 c X T T Q X N0 X N1 l X X G', 'H3 X X X h0 m h1 Q T h3 T Z2 Z1 H2 Z3 h2 N1 Z0 N0 G', 'A2 H3 X X Z0 T T Q A1 h1 Z1 h3 H2 h0 A3 Z2 h2 Z3 T T N1 Q G A0 N0', 'A0 X h1 X X h0 A3 H2 Z0 h2 H3 h3 Z2 Z3 Z1 T A1 T J N1 X N0 O0 Q A2 G O1', 'A0 X h1 X X h0 A3 H2 Z0 h2 H3 h3 Z2 Z3 Z1 T A1 T J N1 X N0 O0 Q A2 G O1', 'A0 X h1 X X h0 A3 H2 Z0 h2 H3 h3 Z2 Z3 Z1 T A1 T J N1 X N0 O0 Q A2 G O1', 'A0 X h1 X X h0 A3 H2 Z0 h2 H3 h3 Z2 Z3 Z1 T A1 T J N1 X N0 O0 Q A2 G O1', 'A1 X h1 Z3 H2 X O0 Z0 A2 h2 H3 h0 Z2 Z1 h3 J G X O1 A0 T A3', 'T R2 T R3 O1 A1 X Z1 X Z2 y5 Z3 y6 X y7 Z0 y4 y3 T y1 y0 A0 R2 R3 O0 J K y2', 'A1 A0 R3 k0 k2 k3 k1 R2 O1 R3 O0 R2', 'T Q R3 T R2 R2 O0 R3 T X O1', 'O0 T R2 O1 R3 F0 R2 R3 F1 F3 F2')


def tile_voting_intention_transfer_t2_kernel(
    tc, x, a_words, a_scales, l_words, l_scales, turnout, w_words, w_scales, electorate, base, out
):
    nc = tc.nc
    engines = {"V": nc.vector, "S": nc.scalar, "G": nc.gpsimd, "Q": nc.sync}
    with ExitStack() as ctx:
        keep = ctx.enter_context(tc.tile_pool(name="keep", bufs=1))
        work = ctx.enter_context(tc.tile_pool(name="work", bufs=2))
        psum = ctx.enter_context(tc.psum_pool(name="psum", bufs=1))
        ctx.enter_context(tc.manual_schedule())

        a_rsc = keep.tile([P, 512], U8, align_bytes=64)
        l_rsc = keep.tile([P, 512], U8, align_bytes=64)
        a_sc = keep.tile([P, 512], U8, align_bytes=64)
        l_sc = keep.tile([P, 512], U8, align_bytes=64)
        a_raw = keep.tile([P, 1024], U8, align_bytes=64)
        l_raw = keep.tile([P, 1024], U8, align_bytes=64)
        a_perm = keep.tile([P, 1024], U8, align_bytes=64)
        l_perm = keep.tile([P, 1024], U8, align_bytes=64)
        w_sb = keep.tile([P, R, 1024], U8, align_bytes=64)
        w_sc = keep.tile([P, R, 512], U8, align_bytes=64)
        vec_rows = keep.tile([P, 512], BF16, align_bytes=64)
        vec = keep.tile([P, (R + 1) * 4], F32)
        base_sb = keep.tile([P, J], BF16)
        ident = keep.tile([P, P], F32)
        warm = keep.tile([P, 1], F32)

        nc.vector.memset(vec_rows[:].bitcast(F32), 0.0)
        nc.vector.memset(a_rsc[:].bitcast(I32), 0)
        nc.vector.memset(l_rsc[:].bitcast(I32), 0)
        nc.vector.memset(warm[:], 0.0)
        nc.scalar.activation(out=warm[:], in_=warm[:], func=COPY, scale=1.0)

        x_view = {}
        a_src = a_words.rearrange("g p n -> p (g n)")
        l_src = l_words.rearrange("g p n -> p (g n)")

        def load_x(queue, n):
            chunk = X_CHUNKS[n]
            width = 512 * len(chunk)
            xn = keep.tile([P, 4, width], BF16, name="x_rows%d" % chunk[0], align_bytes=64)
            rows = x[:, 512 * chunk[0] : 512 * chunk[0] + width].rearrange("(p t) c -> p t c", t=4)
            if n == 0:
                for h in range(2):
                    queue.dma_start(out=xn[:, 2 * h : 2 * h + 2, :], in_=rows[:, 2 * h : 2 * h + 2, :])
            else:
                queue.dma_start(out=xn[:], in_=rows)
            for n, r in enumerate(chunk):
                x_view[r] = (xn, 512 * n)

        def load_scales(queue, dst, s):
            for qd in range(4):
                queue.dma_start(
                    out=dst[32 * qd : 32 * qd + 4, :].bitcast(I32), in_=s[0, 4 * qd : 4 * qd + 4, :].bitcast(I32)
                )

        for word in LOADS.split():
            queue, what = engines[word[0]], word[1:]
            if what == "i":
                make_identity(nc, ident[:])
            elif what == "m":
                nc.gpsimd.memset(w_sc[:].rearrange("p g n -> p (g n)").bitcast(I32), 0)
            elif what == "a":
                queue.dma_start(out=a_raw[:], in_=a_src)
            elif what == "l":
                queue.dma_start(out=l_raw[:], in_=l_src)
            elif what == "as":
                load_scales(queue, a_rsc, a_scales)
            elif what == "ls":
                load_scales(queue, l_rsc, l_scales)
            elif what == "t":
                queue.dma_start(out=vec_rows[0:R, :], in_=turnout.rearrange("(r c) -> r c", r=R))
            elif what == "w":
                queue.dma_start(out=w_sb[:], in_=w_words.rearrange("g p n -> p g n"))
            elif what == "ws":
                for qd in range(4):
                    queue.dma_start(
                        out=w_sc[32 * qd : 32 * qd + 4, :, :].bitcast(I32),
                        in_=w_scales[:, 4 * qd : 4 * qd + 4, :].bitcast(I32).rearrange("g q n -> q g n"),
                    )
            elif what == "e":
                queue.dma_start(out=vec_rows[R : R + 1, :], in_=electorate.rearrange("(r c) -> r c", r=1))
            elif what == "b":
                queue.dma_start(out=base_sb[:], in_=base.partition_broadcast(P))
            else:
                load_x(queue, int(what[1:]))

        xt, xq, xs, xtau, hg, hq, hs, zs, zg, zq, zsc, acc = {}, {}, {}, {}, {}, {}, {}, {}, {}, {}, {}, {}
        banks, zbanks = {}, {}

        def transpose(r, b):
            xn, off = x_view[r]
            if b == 0:
                xt[r] = keep.tile([P, 512, 4], BF16, name="xt%d" % r, align_bytes=64)
            words = xn[:].bitcast(F32)
            bank = psum.tile([P, 2, 2, P], F32, name="tp", tag="acc%d" % (b))
            for t in range(2):
                for u in range(2):
                    lo = off // 2
                    nc.tensor.transpose(bank[:, t, u, :], words[:, 2 * b + t, lo + u : lo + 256 : 2], ident[:])
            (nc.vector.tensor_copy if (r, b) in COPY_T else nc.scalar.copy)(
                out=xt[r][:].bitcast(F32)[:, 256 * b : 256 * b + 256, :].rearrange("p (t m) u -> p t m u", t=2),
                in_=bank[:].rearrange("p t u m -> p t m u"),
            )

        def vectors():
            bank = psum.tile([P, 2, P], F32, name="tv", tag="z", bufs=3)
            for u in range(2):
                nc.tensor.transpose(bank[:, u, :], vec_rows[:].bitcast(F32)[:, u::2], ident[:])
            nc.vector.tensor_copy(
                out=vec[:].rearrange("p (r u e) -> p r u e", u=2, e=2),
                in_=bank[:].bitcast(BF16)[:, :, 0 : 2 * (R + 1)].rearrange("p u (r e) -> p r u e", e=2),
            )

        def quantize(codes, scales, grouped, lo, hi):
            nc.vector.quantize_mx(
                out=codes[:, lo:hi].bitcast(FP8X4),
                scales=scales[:, lo:hi],
                in_=grouped[:, lo:hi, :].rearrange("p e t -> p (e t)"),
            )

        def quantize_x(r, lo, hi):
            if lo == 0:
                xq[r] = keep.tile([P, 512], U32, name="xq%d" % r, align_bytes=64)
                xs[r] = keep.tile([P, 512], U8, name="xs%d" % r, align_bytes=64)
            quantize(xq[r], xs[r], xt[r], lo, hi)

        def x_tau(r, q):
            if r not in xtau:
                xtau[r] = work.tile([P, 4, 512], F32, name="xtau", bufs=3, align_bytes=64)
            factor = vec[:, 4 * r + q : 4 * r + q + 1]
            engine = XTAU.get((r, q), "S")
            if engine == "S":
                nc.scalar.activation(out=xtau[r][:, q, :], in_=xt[r][:, :, q], func=COPY, scale=factor)
            else:
                engines[engine].tensor_scalar(
                    out=xtau[r][:, q, :], in0=xt[r][:, :, q], scalar1=factor, scalar2=0.0, op0=MULT, op1=ADD
                )

        def h_mm(r, q):
            bank = psum.tile([P, 4, P], F32, name="hbank", tag="h", bufs=3)
            banks[r, q] = bank
            for t in range(4):
                nc.tensor.matmul_mx(
                    out=bank[:, t, :],
                    lhsT=xq[r][:, P * t : P * t + P].bitcast(FP8X4),
                    lhsT_scale=xs[r][:, P * t : P * t + P],
                    rhs=a_perm[:, 256 * q : 256 * q + 256].bitcast(FP4X4),
                    rhs_scale=a_sc[:, P * q : P * q + P],
                    start=True,
                    stop=True,
                )

        def h_add(r, q):
            if r not in hg:
                hg[r] = work.tile([P, 512, 4], BF16, name="hg", bufs=2, align_bytes=64)
            xn, off = x_view[r]
            source, engine = banks[r, q], nc.vector
            if (r, q) in HPOOL:
                source, engine = work.tile([P, 4, P], F32, name="hs32", align_bytes=64), nc.gpsimd
                nc.scalar.copy(out=source[:], in_=banks[r, q][:])
            engine.tensor_tensor(
                out=hg[r][:, P * q : P * q + P, :].rearrange("p (c i) t -> p c t i", i=2),
                in0=source[:].rearrange("p t (c i) -> p c t i", i=2),
                in1=xn[:, :, off : off + 512].rearrange("p t (c i q) -> p q c t i", q=4, i=2)[:, q],
                op=ADD,
            )

        def quantize_h(r):
            hq[r] = work.tile([P, 512], U32, name="hq", bufs=2, align_bytes=64)
            hs[r] = work.tile([P, 512], U8, name="hs", bufs=2, align_bytes=64)
            quantize(hq[r], hs[r], hg[r], 0, 512)

        def z_mm(r, q):
            bank = psum.tile([P, 512], F32, name="zbank", tag="h" if 1 and r == R - 1 and q >= 3 else "z", bufs=3)
            zbanks[r, q] = bank
            if r not in zs:
                zs[r] = work.tile([P, 4, 512], F32, name="zs", bufs=3, align_bytes=64)
            nc.tensor.matmul_mx(
                out=bank[:],
                lhsT=a_perm[:, 256 * q : 256 * q + 256].bitcast(FP4X4),
                lhsT_scale=a_sc[:, P * q : P * q + P],
                rhs=xq[r][:].bitcast(FP8X4),
                rhs_scale=xs[r][:],
                start=True,
                stop=False,
            )
            nc.tensor.matmul_mx(
                out=bank[:],
                lhsT=hq[r][:, P * q : P * q + P].bitcast(FP8X4),
                lhsT_scale=hs[r][:, P * q : P * q + P],
                rhs=l_perm[:].bitcast(FP4X4),
                rhs_scale=l_sc[:],
                start=False,
                stop=True,
            )
            if not (1 and r == R - 1):
                z_out(r, q, 0, 512)

        def z_out(r, q, lo, hi):
            k = 4 * r + q
            nc.scalar.activation(
                out=zs[r][:, q, lo:hi], in_=zbanks[r, q][:, lo:hi], func=COPY, scale=vec[:, k : k + 1]
            )

        def z_piece(r, n):
            if n >= len(PIECES[r]):
                return
            if r not in zg:
                zg[r] = work.tile([P, 512, 4], BF16, name="zg", align_bytes=64)
            name, lo, hi = PIECES[r][n]
            engines[name].tensor_tensor(
                out=zg[r][:, lo:hi, :].rearrange("p (c i) q -> p c q i", i=4),
                in0=zs[r][:, :, lo:hi].rearrange("p q (c i) -> p c q i", i=4),
                in1=xtau[r][:, :, lo:hi].rearrange("p q (c i) -> p c q i", i=4),
                op=ADD,
            )

        def quantize_z(r, lo, hi):
            if r not in zq:
                zq[r] = work.tile([P, 512], U32, name="zq", bufs=8, align_bytes=64)
                zsc[r] = work.tile([P, 512], U8, name="zsc", bufs=8, align_bytes=64)
            quantize(zq[r], zsc[r], zg[r], lo, hi)

        def o_mm(r, t):
            if t not in acc:
                acc[t] = psum.tile([P, 512], F32, name="acc", tag="acc%d" % t if t < 2 else "h", bufs=1 if t < 2 else 3)
            nc.tensor.matmul_mx(
                out=acc[t][:],
                lhsT=zq[r][:, P * t : P * t + P].bitcast(FP8X4),
                lhsT_scale=zsc[r][:, P * t : P * t + P],
                rhs=w_sb[:, r, :].bitcast(FP4X4),
                rhs_scale=w_sc[:, r, :],
                start=(r == 0),
                stop=(r == R - 1),
            )

        out_rows = out.rearrange("(m t) j -> t m j", t=4)

        def finish(t):
            o_sb = work.tile([P, J], F32, name="o_sb", bufs=4)
            if t in FIN:
                y_sb = work.tile([P, J], F32, name="y_sb", bufs=2)
                nc.scalar.activation(out=y_sb[:], in_=acc[t][:], func=COPY, scale=vec[:, 4 * R + t : 4 * R + t + 1])
                nc.gpsimd.tensor_tensor(out=o_sb[:], in0=y_sb[:], in1=base_sb[:], op=ADD)
            else:
                nc.vector.scalar_tensor_tensor(
                    out=o_sb[:], in0=acc[t][:], scalar=vec[:, 4 * R + t : 4 * R + t + 1], in1=base_sb[:], op0=MULT, op1=ADD
                )
            nc.sync.dma_start(out=out_rows[t], in_=o_sb[:])

        def permute_words(dst, src):
            nc.vector.tensor_copy(
                out=dst[:].rearrange("p (q m b) -> p q m b", q=4, b=2),
                in_=src[:].rearrange("p (m q b) -> p q m b", q=4, b=2),
            )

        def permute_scales(dst, src):
            nc.vector.tensor_copy(
                out=dst[:].rearrange("p (q m) -> p q m", q=4), in_=src[:].rearrange("p (m q) -> p q m", q=4)
            )

        late = {2: 0, 3: 0}
        counters = {"T": 0, "Q": 0, "X": 0}
        queues = {
            "T": [(r, b) for r in range(R) for b in range(2)],
            "Q": [(0, 0, 256), (0, 256, 512)] + [(r, 0, 512) for r in range(1, R)],
            "X": [(r, q) for r in range(R) for q in range(4)],
        }

        def run(c, k, i):
            if c in counters:
                n = counters[c]
                if n < len(queues[c]):
                    counters[c] = n + 1
                    {"T": transpose, "Q": quantize_x, "X": x_tau}[c](*queues[c][n])
            elif c == "H":
                h_mm(i, k)
            elif c == "N":
                if i + 1 < R:
                    h_mm(i + 1, k)
            elif c == "h":
                h_add(i, k)
            elif c == "G":
                quantize_h(i)
            elif c == "Z":
                z_mm(i - 1, k)
            elif c == "A":
                z_piece(i - 2, k)
            elif c == "B":
                if i > 2:
                    z_piece(i - 3, k)
            elif c == "K":
                quantize_z(i - 2, 0, 512)
            elif c == "J":
                if i > 2:
                    quantize_z(i - 3, 0, 512)
            elif c == "k":
                quantize_z(i - 2, P * k, P * k + P)
            elif c == "O":
                if i > 3:
                    o_mm(i - 4, k)
            elif c == "R":
                o_mm(late[k], k)
                late[k] += 1
            elif c == "F":
                finish(k)
            elif c == "a":
                permute_words(a_perm, a_raw)
            elif c == "b":
                permute_scales(a_sc, a_rsc)
            elif c == "l":
                permute_words(l_perm, l_raw)
            elif c == "m":
                permute_scales(l_sc, l_rsc)
            elif c == "y":
                z_out(R - 1, k % 4, 256 * (k // 4), 256 * (k // 4) + 256)
            elif c == "c":
                vectors()

        for i in range(R + 4):
            for word in STEPS[i].split():
                run(word[0], int(word[1:] or 0), i)
